import numpy as np
import ml_dtypes


def mxq(x, axis, fmt="e4m3"):
    dtype, down = {"e4m3": (ml_dtypes.float8_e4m3fn, 7), "e5m2": (ml_dtypes.float8_e5m2, 14)}[fmt]
    v = np.moveaxis(np.asarray(x, np.float32).astype(ml_dtypes.bfloat16).astype(np.float64), axis, -1)
    blocks = v.reshape(v.shape[:-1] + (-1, 32))
    amax = np.abs(blocks).max(-1, keepdims=True)
    byte = np.maximum(np.where(amax > 0, np.frexp(amax)[1] - 1 + 127, 0) - down, 1)
    scale = np.exp2(byte - 127.0)
    codes = (blocks / scale).astype(np.float32).astype(dtype).astype(np.float64)
    return np.moveaxis((codes * scale).reshape(v.shape), -1, axis)


WIDE = False


def mx_kscale(k):
    if not WIDE:
        return np.ones(k)
    levels = np.array([24, -24, 12, -12, 0])
    if k % 512:
        return np.exp2(np.random.permutation(np.resize(levels, k // 32))).repeat(32)
    a = np.empty((k // 512, 16))
    for p in range(k // 512):
        a[p, :8] = np.random.permutation(np.resize(levels, 8))
        for g in range(8):
            far = levels[np.abs(levels - a[p, g]) >= 10]
            a[p, g + 8] = far[np.random.randint(len(far))]
    return np.exp2(a.ravel()).repeat(32)


def f64(x):
    return np.asarray(x).astype(np.float64)


def striped8(idx):
    return np.concatenate([v.reshape(-1, 16).T for v in idx]).astype(np.uint16)


def unstriped8(offs):
    return np.stack([offs[16 * g:16 * g + 16].T.reshape(-1) for g in range(8)]).astype(np.int64)


E2M1 = np.array([0.0, 0.5, 1.0, 1.5, 2.0, 3.0, 4.0, 6.0, -0.0, -0.5, -1.0, -1.5, -2.0, -3.0, -4.0, -6.0])


def pack_weight(w, fmt):
    k, n = w.shape
    w = f64(np.asarray(w, np.float32).astype(ml_dtypes.bfloat16)).reshape(k // 32, 32, n)
    amax = np.abs(w).max(1)
    if fmt == "e4m3":
        byte = np.frexp(amax)[1] - 1 + 127 - 7
    else:
        mant, ex = np.frexp(amax / 6.0)
        byte = np.where(mant > 0.5, ex, ex - 1) + 127
    byte = np.clip(np.where(amax > 0, byte, 1), 1, 254)
    scaled = (w * np.exp2(127.0 - byte)[:, None, :]).reshape(k, n).astype(np.float32)
    by_word = np.ascontiguousarray(scaled.reshape(k // 512, 128, 4, n).transpose(0, 1, 3, 2))
    if fmt == "e4m3":
        words = by_word.astype(ml_dtypes.float8_e4m3fn).view(np.uint8)
    else:
        c = by_word.astype(ml_dtypes.float4_e2m1fn).view(np.uint8) & 0xF
        words = (c[..., 0::2] | (c[..., 1::2] << 4)).reshape(k // 512, 128, 2 * n)
    return np.ascontiguousarray(words), np.ascontiguousarray(byte.astype(np.uint8).reshape(k // 512, 16, n))


def unpack_weight(words, scales, fmt):
    g, _, n = scales.shape
    words = np.ascontiguousarray(words).reshape(g, 128, n, -1)
    if fmt == "e4m3":
        vals = words.view(ml_dtypes.float8_e4m3fn).astype(np.float64)
    else:
        nib = np.empty((g, 128, n, 4), np.uint8)
        nib[..., 0::2] = words & 0xF
        nib[..., 1::2] = words >> 4
        vals = E2M1[nib]
    vals = vals * np.repeat(np.exp2(scales.astype(np.float64) - 127.0), 8, axis=1)[..., None]
    return vals.transpose(0, 1, 3, 2).reshape(g * 512, n)


def planes(y):
    n, m = y.shape
    v = y.astype(np.float32).astype(ml_dtypes.bfloat16).astype(np.float64).reshape(n // 32, 32, m)
    top = np.abs(v).max(1)
    byte = np.clip(np.where(top > 0, np.frexp(top)[1] - 1 + 127 - 7, 1), 1, 254)
    codes = (v * np.exp2(127.0 - byte)[:, None, :]).reshape(n, m).astype(np.float32).astype(ml_dtypes.float8_e4m3fn).view(np.uint8)
    words = codes.reshape(n // 512, 128, 4, m).transpose(0, 1, 3, 2)
    return np.ascontiguousarray(words), np.ascontiguousarray(byte.astype(np.uint8).reshape(n // 512, 16, m))


K, N, T, J = 512, 512, 2048, 512


def setup_inputs():
    n = np.random.standard_normal
    s = mx_kscale(K)[:, None]
    p_w4 = pack_weight(n((K, N)) / np.sqrt(K) / s, "e2m1")
    return {
        "xT": (n((K, T)) * s).astype(np.float32),
        "wgt": np.repeat(np.random.uniform(0.5, 2.0, (8, 3 * J)), 16, axis=0).astype(np.float32),
        "w4_words": p_w4[0],
        "w4_scales": p_w4[1],
        "wd": (0.4 * (n((K, N)) / np.sqrt(K) / s)).astype(np.float32),
        "iw0": (np.random.uniform(0.1, 0.9, (N, J))).astype(np.float32),
        "iw1": (np.random.uniform(0.1, 0.9, (N, J))).astype(np.float32),
        "iw2": (np.random.uniform(0.1, 0.9, (N, J))).astype(np.float32),
        "b": (0.3 * n(N)).astype(np.float32),
        "offs": striped8(np.stack([np.concatenate([np.random.permutation(T)[:J] for _ in range(3)]) for _ in range(8)])),
    }


def reference(xT, wgt, w4_words, w4_scales, wd, iw0, iw1, iw2, b, offs):
    idx = unstriped8(offs)
    rows = np.arange(K)
    xg = f64(wgt)[rows // 4 % 128] * f64(xT)[rows[:, None], idx[rows % 512 // 64]]
    xT_ = mxq(xg, 0, "e4m3").reshape(K, 3, J)
    w4_ = unpack_weight(w4_words, w4_scales, "e2m1")
    wd_ = mxq(f64(wd), 0, "e4m3")
    a0 = w4_.T @ xT_[:, 0] + wd_.T @ xT_[:, 0]
    a1 = w4_.T @ xT_[:, 1] + wd_.T @ xT_[:, 1]
    a2 = w4_.T @ xT_[:, 2] + wd_.T @ xT_[:, 2]
    out_0 = a0 * f64(iw0) + a1 * f64(iw1) + a2 * f64(iw2) + f64(b)[:, None]
    return (out_0,) + planes(out_0)

@@ -1,0 +1,216 @@
+from contextlib import ExitStack
+
+import concourse.mybir as mybir
+from concourse.masks import make_identity
+
+FLOPS = 1610612736
+
+F32 = mybir.dt.float32
+BF16 = mybir.dt.bfloat16
+I32 = mybir.dt.int32
+U32 = mybir.dt.uint32
+U16 = mybir.dt.uint16
+U8 = mybir.dt.uint8
+FP8X4 = mybir.dt.float8_e4m3fn_x4
+FP4X4 = mybir.dt.float4_e2m1fn_x4
+MULT = mybir.AluOpType.mult
+ADD = mybir.AluOpType.add
+IDENTITY = mybir.ActivationFunctionType.Identity
+
+P = 128
+PACK = 4
+N = 512
+T = 2048
+J = 512
+PICKS = 3
+LIST_ROWS = 16
+BANK = 512
+
+SEGMENTS = ((0, 256, "tensor"), (256, 256, "vector"))
+AHEAD = 3
+
+
+def tile_list_dl_soft_biasP_kernel(
+    tc, xT, wgt, w4_words, w4_scales, wd, iw0, iw1, iw2, b, offs, out_0, out_1, out_2
+):
+    nc = tc.nc
+    iw = (iw0, iw1, iw2)
+    units = [(seg, c) for seg in SEGMENTS for c in range(PICKS)]
+
+    with ExitStack() as ctx:
+        keep = ctx.enter_context(tc.tile_pool(name="keep", bufs=1))
+        psum = ctx.enter_context(tc.psum_pool(name="psum", bufs=1))
+
+        offsets = keep.tile([P, PICKS * J // LIST_ROWS], U16, name="offsets")
+        nc.sync.dma_start(offsets[:], offs)
+
+        w4_raw = keep.tile([P, 2 * N], U8, name="w4_raw")
+        nc.sync.dma_start(w4_raw[:].bitcast(I32), w4_words[0].bitcast(I32))
+        s4_raw = keep.tile([P, N], U8, name="s4_raw")
+        nc.vector.memset(s4_raw[:].bitcast(I32), 0)
+        for q in range(4):
+            nc.scalar.dma_start(s4_raw[32 * q : 32 * q + 4, :].bitcast(I32), w4_scales[0, 4 * q : 4 * q + 4, :].bitcast(I32))
+
+        x_planes = xT.rearrange("(p i) t -> p i t", i=PACK)
+        wgt_sb = [keep.tile([P, J], F32, name=f"wgt{c}") for c in range(PICKS)]
+        plane = [keep.tile([P, T], F32, name=f"plane{i}") for i in range(PACK)]
+        wd_raw = keep.tile([P, PACK, N], F32, name="wd_raw")
+        bias = keep.tile([P, PACK], F32, name="bias")
+        nc.sync.dma_start(wgt_sb[0][:], wgt[:, 0:J])
+        nc.sync.dma_start(plane[0][:], x_planes[:, 0, :])
+        for c in range(1, PICKS):
+            nc.sync.dma_start(wgt_sb[c][:], wgt[:, c * J : (c + 1) * J])
+        nc.sync.dma_start(plane[1][:], x_planes[:, 1, :])
+        nc.sync.dma_start(wd_raw[:], wd.rearrange("(p i) n -> p i n", i=PACK))
+        nc.sync.dma_start(plane[2][:], x_planes[:, 2, :])
+        nc.sync.dma_start(plane[3][:], x_planes[:, 3, :])
+        iw_sb = []
+        for u, ((j0, w, mode), c) in enumerate(units):
+            t_iw = keep.tile([P, PACK, w], F32, name=f"iw{u}")
+            nc.sync.dma_start(t_iw[:], iw[c].rearrange("(p t) j -> p t j", t=PACK)[:, :, j0 : j0 + w])
+            iw_sb.append(t_iw)
+        nc.sync.dma_start(bias[:], b.rearrange("(p t) -> p t", t=PACK))
+
+        ident = keep.tile([P, P], F32, name="ident")
+        make_identity(nc, ident[:])
+
+        w4_codes = keep.tile([P, 2 * N], U8, name="w4_codes", align_bytes=64)
+        nc.vector.tensor_copy(
+            w4_codes[:].rearrange("p (t m e) -> p t m e", t=PACK, e=2),
+            w4_raw[:].rearrange("p (m t e) -> p t m e", t=PACK, e=2),
+        )
+        w4_plane = keep.tile([P, N], U8, name="w4_plane", align_bytes=64)
+        nc.vector.tensor_copy(
+            w4_plane[:].rearrange("p (t m) -> p t m", t=PACK),
+            s4_raw[:].rearrange("p (m t) -> p t m", t=PACK),
+        )
+
+        def gather(dst, i, c, j0, w):
+            first = (c * J + j0) // LIST_ROWS
+            picks = offsets[:, first : first + w // LIST_ROWS]
+            nc.vector.tensor_tensor(dst, plane[i][:].indirect(picks), wgt_sb[c][:, j0 : j0 + w], MULT)
+
+        low = [keep.tile([P, 2, J], F32, name=f"low{c}") for c in range(PICKS)]
+        for i in range(2):
+            for c in range(PICKS):
+                gather(low[c][:, i, :], i, c, 0, J)
+
+        wd_bf = keep.tile([P, PACK, P, PACK], BF16, name="wd_bf", align_bytes=64)
+        nc.scalar.copy(
+            wd_bf[:].rearrange("p t m i -> p m t i"),
+            wd_raw[:].rearrange("p i (m t) -> p m t i", t=PACK),
+        )
+        wd_codes = keep.tile([P, N], U32, name="wd_codes", align_bytes=64)
+        wd_plane = keep.tile([P, N], U8, name="wd_plane", align_bytes=64)
+        nc.vector.quantize_mx(wd_codes[:].bitcast(FP8X4), wd_plane[:], wd_bf[:].rearrange("p t m i -> p (t m i)"))
+
+        xg_bf = {}
+
+        y_plane = keep.tile([P, J], U8, name="y_plane", align_bytes=64)
+        y_rows = out_0.rearrange("(p t) j -> p t j", t=PACK)
+        y_words = out_1[0].rearrange("p j i -> p (j i)").bitcast(I32)
+        banks = {}
+        prods = {}
+        sums_t = {}
+
+        def pick(u):
+            (j0, w, mode), c = units[u]
+            xg_bf[u] = keep.tile([P, w, PACK], BF16, name=f"xg_bf{u}", tag=f"slot{u}", align_bytes=64)
+            nc.scalar.copy(xg_bf[u][:, :, 0:2], low[c][:, :, j0 : j0 + w].rearrange("p i j -> p j i"))
+            tag = f"slot{u - AHEAD}" if u >= AHEAD else f"first{u}"
+            high = keep.tile([P, 2, w], F32, name=f"high{u}", tag=tag, align_bytes=64)
+            for i in range(2):
+                gather(high[:, i, :], 2 + i, c, j0, w)
+            nc.scalar.copy(xg_bf[u][:, :, 2:4], high[:].rearrange("p i j -> p j i"))
+
+        def project(u):
+            (j0, w, mode), c = units[u]
+            codes = keep.tile([P, w], U32, name=f"xg_codes{u}", align_bytes=64)
+            scales = keep.tile([P, w], U8, name=f"xg_plane{u}", align_bytes=64)
+            nc.vector.quantize_mx(codes[:].bitcast(FP8X4), scales[:], xg_bf[u][:].rearrange("p j i -> p (j i)"))
+            banks[u] = []
+            for h in range(w // P):
+                acc = psum.tile([P, PACK, P], F32, name=f"acc{u}_{h}", tag="acc", bufs=4)
+                banks[u].append(acc)
+                js = slice(h * P, (h + 1) * P)
+                for t in range(PACK):
+                    cols = slice(t * P, (t + 1) * P)
+                    nc.tensor.matmul_mx(
+                        acc[:, t, :], wd_codes[:, cols].bitcast(FP8X4), wd_plane[:, cols],
+                        codes[:, js].bitcast(FP8X4), scales[:, js], start=True, stop=False,
+                    )
+                    nc.tensor.matmul_mx(
+                        acc[:, t, :], w4_codes[:, 2 * t * P : 2 * (t + 1) * P].bitcast(FP4X4), w4_plane[:, cols],
+                        codes[:, js].bitcast(FP8X4), scales[:, js], start=False, stop=True,
+                    )
+
+        def hand_out(seg, y_bf):
+            j0, w, mode = seg
+            y_codes = keep.tile([P, w], U32, name=f"y_codes{j0}", align_bytes=64)
+            nc.vector.quantize_mx(y_codes[:].bitcast(FP8X4), y_plane[:, j0 : j0 + w], y_bf[:].rearrange("p j t -> p (j t)"))
+            nc.sync.dma_start(y_words[:, j0 : j0 + w], y_codes[:].bitcast(I32))
+
+        def pool_up(u):
+            seg, c = units[u]
+            j0, w, mode = seg
+            per_bank = BANK // w
+            last = c == PICKS - 1
+            prod = keep.tile([P, w // P, PACK, P], F32, name=f"prod{u}")
+            if last:
+                y_bf = keep.tile([P, w, PACK], BF16, name=f"y_bf{j0}", align_bytes=64)
+            if mode == "tensor":
+                for h, acc in enumerate(banks[u]):
+                    nc.vector.tensor_tensor(prod[:, h, :, :], acc[:], iw_sb[u][:, :, h * P : (h + 1) * P], MULT)
+                    if c == 0:
+                        sums_t[j0, h] = psum.tile([P, PACK, P], F32, name=f"sum_t{j0}_{h}", tag="sum_t", bufs=2)
+                    for t in range(PACK):
+                        nc.tensor.matmul(
+                            sums_t[j0, h][:, t, :], prod[:, h, t, :], ident[:], is_transpose=True,
+                            start=(c == 0 and t == 0), stop=(last and t == PACK - 1),
+                        )
+                if last:
+                    turned = keep.tile([P, w // P, PACK, P], F32, name=f"turned{j0}")
+                    for h in range(w // P):
+                        nc.scalar.copy(turned[:, h, :, :], sums_t[j0, h][:])
+                    y = keep.tile([P, PACK, w], F32, name=f"y{j0}")
+                    for t in range(PACK):
+                        if t % per_bank == 0:
+                            back = psum.tile([P, per_bank, w], F32, name=f"back{j0}_{t}", tag="back", bufs=2)
+                        for h in range(w // P):
+                            nc.tensor.transpose(back[:, t % per_bank, h * P : (h + 1) * P], turned[:, h, t, :], ident[:])
+                        if t % per_bank == per_bank - 1:
+                            for s in range(per_bank):
+                                row = t - per_bank + 1 + s
+                                nc.scalar.activation(y[:, row, :], back[:, s, :], IDENTITY, bias=bias[:, row : row + 1])
+                    nc.sync.dma_start(y_rows[:, :, j0 : j0 + w], y[:])
+                    nc.scalar.copy(y_bf[:], y[:].rearrange("p t j -> p j t"))
+                    hand_out(seg, y_bf)
+            else:
+                total = keep.tile([P, w // P, PACK, P], F32, name=f"total{u}")
+                for h, acc in enumerate(banks[u]):
+                    js = slice(h * P, (h + 1) * P)
+                    nc.vector.tensor_tensor(prod[:, h, :, :], acc[:], iw_sb[u][:, :, js], MULT)
+                    if c > 0:
+                        nc.vector.tensor_tensor(total[:, h, :, :], prods[u - 1][:, h, :, :], prod[:, h, :, :], ADD)
+                    if last:
+                        nc.sync.dma_start(y_rows[:, :, j0 + h * P : j0 + (h + 1) * P], total[:, h, :, :])
+                        copy = nc.scalar.copy if h < w // P - 1 else nc.vector.tensor_copy
+                        copy(y_bf[:, js, :], total[:, h, :, :].rearrange("p t j -> p j t"))
+                if c == 0:
+                    for t in range(PACK):
+                        nc.scalar.activation(total[:, :, t, :], prod[:, :, t, :], IDENTITY, bias=bias[:, t : t + 1])
+                prods[u] = total
+                if last:
+                    hand_out(seg, y_bf)
+
+        for step in range(len(units) + 2):
+            if step < len(units):
+                pick(step)
+            if 1 <= step <= len(units):
+                project(step - 1)
+            if step >= 2:
+                pool_up(step - 2)
+
+        for q in range(4):
+            queue = nc.sync if q % 2 == 0 else nc.scalar
+            queue.dma_start(out_2[0, 4 * q : 4 * q + 4, :].bitcast(I32), y_plane[32 * q : 32 * q + 4, :].bitcast(I32))

@@ -47,7 +47,7 @@ def tile_list_dl_soft_biasP_kernel(
         w4_raw = keep.tile([P, 2 * N], U8, name="w4_raw")
         nc.sync.dma_start(w4_raw[:].bitcast(I32), w4_words[0].bitcast(I32))
         s4_raw = keep.tile([P, N], U8, name="s4_raw")
-        nc.vector.memset(s4_raw[:].bitcast(I32), 0)
+        nc.gpsimd.memset(s4_raw[:].bitcast(I32), 0)
         for q in range(4):
             nc.scalar.dma_start(s4_raw[32 * q : 32 * q + 4, :].bitcast(I32), w4_scales[0, 4 * q : 4 * q + 4, :].bitcast(I32))
 
@@ -60,19 +60,28 @@ def tile_list_dl_soft_biasP_kernel(
         nc.sync.dma_start(plane[0][:], x_planes[:, 0, :])
         for c in range(1, PICKS):
             nc.sync.dma_start(wgt_sb[c][:], wgt[:, c * J : (c + 1) * J])
+        nc.sync.dma_start(bias[:], b.rearrange("(p t) -> p t", t=PACK))
         nc.sync.dma_start(plane[1][:], x_planes[:, 1, :])
         nc.sync.dma_start(wd_raw[:], wd.rearrange("(p i) n -> p i n", i=PACK))
         nc.sync.dma_start(plane[2][:], x_planes[:, 2, :])
         nc.sync.dma_start(plane[3][:], x_planes[:, 3, :])
         iw_sb = []
         for u, ((j0, w, mode), c) in enumerate(units):
-            t_iw = keep.tile([P, PACK, w], F32, name=f"iw{u}")
+            t_iw = keep.tile([P, PACK, w], F32, name=f"iw{u}", tag=f"iw_slot{u}", align_bytes=64)
             nc.sync.dma_start(t_iw[:], iw[c].rearrange("(p t) j -> p t j", t=PACK)[:, :, j0 : j0 + w])
             iw_sb.append(t_iw)
-        nc.sync.dma_start(bias[:], b.rearrange("(p t) -> p t", t=PACK))
 
         ident = keep.tile([P, P], F32, name="ident")
         make_identity(nc, ident[:])
+        sums_t = []
+        for h in range(J // P):
+            sum_t = psum.tile([P, PACK, P], F32, name=f"sum_t{h}", tag=f"sum{h}")
+            sums_t.append(sum_t)
+            for t in range(PACK):
+                nc.tensor.matmul(
+                    sum_t[:, t, :], bias[:, t : t + 1].to_broadcast([P, P]), ident[:], is_transpose=True,
+                    start=(t == 0), stop=False,
+                )
 
         w4_codes = keep.tile([P, 2 * N], U8, name="w4_codes", align_bytes=64)
         nc.vector.tensor_copy(
@@ -111,13 +120,12 @@ def tile_list_dl_soft_biasP_kernel(
         y_words = out_1[0].rearrange("p j i -> p (j i)").bitcast(I32)
         banks = {}
         prods = {}
-        sums_t = {}
 
         def pick(u):
             (j0, w, mode), c = units[u]
-            xg_bf[u] = keep.tile([P, w, PACK], BF16, name=f"xg_bf{u}", tag=f"slot{u}", align_bytes=64)
+            xg_bf[u] = keep.tile([P, w, PACK], BF16, name=f"xg_bf{u}", tag=(f"slot{u}" if u < 3 else f"first{u - 3}"), align_bytes=64)
             nc.scalar.copy(xg_bf[u][:, :, 0:2], low[c][:, :, j0 : j0 + w].rearrange("p i j -> p j i"))
-            tag = f"slot{u - AHEAD}" if u >= AHEAD else f"first{u}"
+            tag = f"first{u}" if u < 3 else ("slot0" if u == 3 else f"iw_slot{u - 4}")
             high = keep.tile([P, 2, w], F32, name=f"high{u}", tag=tag, align_bytes=64)
             for i in range(2):
                 gather(high[:, i, :], 2 + i, c, j0, w)
@@ -147,61 +155,53 @@ def tile_list_dl_soft_biasP_kernel(
         def hand_out(seg, y_bf):
             j0, w, mode = seg
             y_codes = keep.tile([P, w], U32, name=f"y_codes{j0}", align_bytes=64)
-            nc.vector.quantize_mx(y_codes[:].bitcast(FP8X4), y_plane[:, j0 : j0 + w], y_bf[:].rearrange("p j t -> p (j t)"))
+            piece = w if mode == "tensor" else P
+            for first in range(0, w, piece):
+                js = slice(first, first + piece)
+                nc.vector.quantize_mx(
+                    y_codes[:, js].bitcast(FP8X4), y_plane[:, j0 + first : j0 + first + piece],
+                    y_bf[:, js, :].rearrange("p j t -> p (j t)"),
+                )
             nc.sync.dma_start(y_words[:, j0 : j0 + w], y_codes[:].bitcast(I32))
 
         def pool_up(u):
             seg, c = units[u]
             j0, w, mode = seg
-            per_bank = BANK // w
             last = c == PICKS - 1
+            closing = PICKS - 1 if mode == "tensor" else PICKS - 2
             prod = keep.tile([P, w // P, PACK, P], F32, name=f"prod{u}")
             if last:
+                y = keep.tile([P, PACK, w], F32, name=f"y{j0}")
                 y_bf = keep.tile([P, w, PACK], BF16, name=f"y_bf{j0}", align_bytes=64)
-            if mode == "tensor":
-                for h, acc in enumerate(banks[u]):
-                    nc.vector.tensor_tensor(prod[:, h, :, :], acc[:], iw_sb[u][:, :, h * P : (h + 1) * P], MULT)
-                    if c == 0:
-                        sums_t[j0, h] = psum.tile([P, PACK, P], F32, name=f"sum_t{j0}_{h}", tag="sum_t", bufs=2)
+            for h, acc in enumerate(banks[u]):
+                js = slice(h * P, (h + 1) * P)
+                tile_j = j0 // P + h
+                nc.vector.tensor_tensor(prod[:, h, :, :], acc[:], iw_sb[u][:, :, js], MULT)
+                if c <= closing:
                     for t in range(PACK):
                         nc.tensor.matmul(
-                            sums_t[j0, h][:, t, :], prod[:, h, t, :], ident[:], is_transpose=True,
-                            start=(c == 0 and t == 0), stop=(last and t == PACK - 1),
+                            sums_t[tile_j][:, t, :], prod[:, h, t, :], ident[:], is_transpose=True,
+                            start=False, stop=(c == closing and t == PACK - 1),
                         )
-                if last:
-                    turned = keep.tile([P, w // P, PACK, P], F32, name=f"turned{j0}")
-                    for h in range(w // P):
-                        nc.scalar.copy(turned[:, h, :, :], sums_t[j0, h][:])
-                    y = keep.tile([P, PACK, w], F32, name=f"y{j0}")
+                if c == closing:
+                    turned = keep.tile([P, PACK, P], F32, name=f"turned{tile_j}")
+                    nc.scalar.copy(turned[:], sums_t[tile_j][:])
+                    back = psum.tile([P, PACK, P], F32, name=f"back{tile_j}", tag=f"sum{tile_j}")
+                    prods[tile_j] = back
                     for t in range(PACK):
-                        if t % per_bank == 0:
-                            back = psum.tile([P, per_bank, w], F32, name=f"back{j0}_{t}", tag="back", bufs=2)
-                        for h in range(w // P):
-                            nc.tensor.transpose(back[:, t % per_bank, h * P : (h + 1) * P], turned[:, h, t, :], ident[:])
-                        if t % per_bank == per_bank - 1:
-                            for s in range(per_bank):
-                                row = t - per_bank + 1 + s
-                                nc.scalar.activation(y[:, row, :], back[:, s, :], IDENTITY, bias=bias[:, row : row + 1])
+                        nc.tensor.transpose(back[:, t, :], turned[:, t, :], ident[:])
+                if last:
+                    if mode == "tensor":
+                        nc.scalar.copy(y[:, :, js], prods[tile_j][:])
+                    else:
+                        nc.vector.tensor_tensor(y[:, :, js], prods[tile_j][:], prod[:, h, :, :], ADD)
+                        nc.sync.dma_start(y_rows[:, :, j0 + h * P : j0 + (h + 1) * P], y[:, :, js])
+                    copy = nc.vector.tensor_copy if tile_j == J // P - 1 else nc.scalar.copy
+                    copy(y_bf[:, js, :], y[:, :, js].rearrange("p t j -> p j t"))
+            if last:
+                if mode == "tensor":
                     nc.sync.dma_start(y_rows[:, :, j0 : j0 + w], y[:])
-                    nc.scalar.copy(y_bf[:], y[:].rearrange("p t j -> p j t"))
-                    hand_out(seg, y_bf)
-            else:
-                total = keep.tile([P, w // P, PACK, P], F32, name=f"total{u}")
-                for h, acc in enumerate(banks[u]):
-                    js = slice(h * P, (h + 1) * P)
-                    nc.vector.tensor_tensor(prod[:, h, :, :], acc[:], iw_sb[u][:, :, js], MULT)
-                    if c > 0:
-                        nc.vector.tensor_tensor(total[:, h, :, :], prods[u - 1][:, h, :, :], prod[:, h, :, :], ADD)
-                    if last:
-                        nc.sync.dma_start(y_rows[:, :, j0 + h * P : j0 + (h + 1) * P], total[:, h, :, :])
-                        copy = nc.scalar.copy if h < w // P - 1 else nc.vector.tensor_copy
-                        copy(y_bf[:, js, :], total[:, h, :, :].rearrange("p t j -> p j t"))
-                if c == 0:
-                    for t in range(PACK):
-                        nc.scalar.activation(total[:, :, t, :], prod[:, :, t, :], IDENTITY, bias=bias[:, t : t + 1])
-                prods[u] = total
-                if last:
-                    hand_out(seg, y_bf)
+                hand_out(seg, y_bf)
 
         for step in range(len(units) + 2):
             if step < len(units):

@@ -43,25 +43,29 @@ def tile_list_dl_soft_biasP_kernel(
 
         offsets = keep.tile([P, PICKS * J // LIST_ROWS], U16, name="offsets")
         nc.sync.dma_start(offsets[:], offs)
+        s4_raw = keep.tile([P, N], U8, name="s4_raw")
+        nc.vector.memset(s4_raw[:].bitcast(I32), 0)
+        wgt_pieces = wgt.rearrange("(g q) (r m) -> g q r m", q=LIST_ROWS, m=P)[:, 0, :, :]
+        wgt_rows = [keep.tile([P, P], F32, name=f"wgt_rows{k}") for k in range(2)]
+        nc.vector.memset(wgt_rows[0][64:128, :], 0.0)
+        nc.vector.memset(wgt_rows[1][32:64, :], 0.0)
+        nc.vector.memset(wgt_rows[1][64:128, :], 0.0)
+        nc.sync.dma_start(wgt_rows[0][0:64, :], wgt_pieces[:, 0:8, :])
 
         w4_raw = keep.tile([P, 2 * N], U8, name="w4_raw")
         nc.sync.dma_start(w4_raw[:].bitcast(I32), w4_words[0].bitcast(I32))
-        s4_raw = keep.tile([P, N], U8, name="s4_raw")
-        nc.gpsimd.memset(s4_raw[:].bitcast(I32), 0)
-        for q in range(4):
-            nc.scalar.dma_start(s4_raw[32 * q : 32 * q + 4, :].bitcast(I32), w4_scales[0, 4 * q : 4 * q + 4, :].bitcast(I32))
 
         x_planes = xT.rearrange("(p i) t -> p i t", i=PACK)
         wgt_sb = [keep.tile([P, J], F32, name=f"wgt{c}") for c in range(PICKS)]
         plane = [keep.tile([P, T], F32, name=f"plane{i}") for i in range(PACK)]
         wd_raw = keep.tile([P, PACK, N], F32, name="wd_raw")
         bias = keep.tile([P, PACK], F32, name="bias")
-        nc.sync.dma_start(wgt_sb[0][:], wgt[:, 0:J])
         nc.sync.dma_start(plane[0][:], x_planes[:, 0, :])
-        for c in range(1, PICKS):
-            nc.sync.dma_start(wgt_sb[c][:], wgt[:, c * J : (c + 1) * J])
+        nc.sync.dma_start(wgt_rows[1][0:32, :], wgt_pieces[:, 8:12, :])
         nc.sync.dma_start(bias[:], b.rearrange("(p t) -> p t", t=PACK))
         nc.sync.dma_start(plane[1][:], x_planes[:, 1, :])
+        for q in range(4):
+            nc.sync.dma_start(s4_raw[32 * q : 32 * q + 4, :].bitcast(I32), w4_scales[0, 4 * q : 4 * q + 4, :].bitcast(I32))
         nc.sync.dma_start(wd_raw[:], wd.rearrange("(p i) n -> p i n", i=PACK))
         nc.sync.dma_start(plane[2][:], x_planes[:, 2, :])
         nc.sync.dma_start(plane[3][:], x_planes[:, 3, :])
@@ -73,8 +77,23 @@ def tile_list_dl_soft_biasP_kernel(
 
         ident = keep.tile([P, P], F32, name="ident")
         make_identity(nc, ident[:])
+        warm = keep.tile([P, 1], F32, name="warm")
+        nc.scalar.copy(warm[:], ident[:, 0:1])
+
+        for c in range(PICKS):
+            if c % 2 == 0:
+                by_place = psum.tile([P, P], F32, name=f"by_place{c}", tag="sum0")
+                nc.tensor.transpose(by_place[:], wgt_rows[c // 2][:], ident[:])
+                runs = 8 if c == 0 else 4
+                pieces = by_place[:, 0 : 8 * runs].rearrange("m (g r) -> m r g", r=runs)
+            spread = keep.tile([P, PACK, 8, LIST_ROWS], F32, name=f"spread{c}")
+            nc.scalar.copy(spread[:], pieces[:, PACK * (c % 2) : PACK * (c % 2 + 1), :].unsqueeze(3).to_broadcast([P, PACK, 8, LIST_ROWS]))
+            turned_back = psum.tile([P, PACK, P], F32, name=f"wgt_ps{c}", tag="sum1")
+            for r in range(PACK):
+                nc.tensor.transpose(turned_back[:, r, :], spread[:, r, :, :].rearrange("m g q -> m (g q)"), ident[:])
+            nc.scalar.copy(wgt_sb[c][:], turned_back[:].rearrange("p r m -> p (r m)"))
         sums_t = []
-        for h in range(J // P):
+        for h in range(2):
             sum_t = psum.tile([P, PACK, P], F32, name=f"sum_t{h}", tag=f"sum{h}")
             sums_t.append(sum_t)
             for t in range(PACK):
@@ -87,11 +106,6 @@ def tile_list_dl_soft_biasP_kernel(
         nc.vector.tensor_copy(
             w4_codes[:].rearrange("p (t m e) -> p t m e", t=PACK, e=2),
             w4_raw[:].rearrange("p (m t e) -> p t m e", t=PACK, e=2),
-        )
-        w4_plane = keep.tile([P, N], U8, name="w4_plane", align_bytes=64)
-        nc.vector.tensor_copy(
-            w4_plane[:].rearrange("p (t m) -> p t m", t=PACK),
-            s4_raw[:].rearrange("p (m t) -> p t m", t=PACK),
         )
 
         def gather(dst, i, c, j0, w):
@@ -113,32 +127,43 @@ def tile_list_dl_soft_biasP_kernel(
         wd_plane = keep.tile([P, N], U8, name="wd_plane", align_bytes=64)
         nc.vector.quantize_mx(wd_codes[:].bitcast(FP8X4), wd_plane[:], wd_bf[:].rearrange("p t m i -> p (t m i)"))
 
+        w4_plane = keep.tile([P, N], U8, name="w4_plane", tag="wd_bf", align_bytes=64)
+        nc.vector.tensor_copy(
+            w4_plane[:].rearrange("p (t m) -> p t m", t=PACK),
+            s4_raw[:].rearrange("p (m t) -> p t m", t=PACK),
+        )
         xg_bf = {}
 
         y_plane = keep.tile([P, J], U8, name="y_plane", align_bytes=64)
         y_rows = out_0.rearrange("(p t) j -> p t j", t=PACK)
         y_words = out_1[0].rearrange("p j i -> p (j i)").bitcast(I32)
         banks = {}
+        quantised = {}
         prods = {}
 
         def pick(u):
             (j0, w, mode), c = units[u]
-            xg_bf[u] = keep.tile([P, w, PACK], BF16, name=f"xg_bf{u}", tag=(f"slot{u}" if u < 3 else f"first{u - 3}"), align_bytes=64)
+            xg_bf[u] = keep.tile([P, w, PACK], BF16, name=f"xg_bf{u}", tag=("slot0", "slot1", "slot2", "first1", "first0", "slot2")[u], align_bytes=64)
             nc.scalar.copy(xg_bf[u][:, :, 0:2], low[c][:, :, j0 : j0 + w].rearrange("p i j -> p j i"))
-            tag = f"first{u}" if u < 3 else ("slot0" if u == 3 else f"iw_slot{u - 4}")
+            tag = ("first0", "first1", "first0", "slot1", "iw_slot0", "iw_slot1")[u]
             high = keep.tile([P, 2, w], F32, name=f"high{u}", tag=tag, align_bytes=64)
             for i in range(2):
                 gather(high[:, i, :], 2 + i, c, j0, w)
             nc.scalar.copy(xg_bf[u][:, :, 2:4], high[:].rearrange("p i j -> p j i"))
 
-        def project(u):
+        def quantise(u):
             (j0, w, mode), c = units[u]
             codes = keep.tile([P, w], U32, name=f"xg_codes{u}", align_bytes=64)
             scales = keep.tile([P, w], U8, name=f"xg_plane{u}", align_bytes=64)
             nc.vector.quantize_mx(codes[:].bitcast(FP8X4), scales[:], xg_bf[u][:].rearrange("p j i -> p (j i)"))
+            quantised[u] = (codes, scales)
+
+        def project(u):
+            (j0, w, mode), c = units[u]
+            codes, scales = quantised[u]
             banks[u] = []
             for h in range(w // P):
-                acc = psum.tile([P, PACK, P], F32, name=f"acc{u}_{h}", tag="acc", bufs=4)
+                acc = psum.tile([P, PACK, P], F32, name=f"acc{u}_{h}", tag="acc", bufs=6)
                 banks[u].append(acc)
                 js = slice(h * P, (h + 1) * P)
                 for t in range(PACK):
@@ -164,52 +189,69 @@ def tile_list_dl_soft_biasP_kernel(
                 )
             nc.sync.dma_start(y_words[:, j0 : j0 + w], y_codes[:].bitcast(I32))
 
+        def turn_back(seg):
+            j0, w, mode = seg
+            y = keep.tile([P, PACK, w], F32, name=f"y{j0}")
+            y_bf = keep.tile([P, w, PACK], BF16, name=f"y_bf{j0}", align_bytes=64)
+            for h in range(w // P):
+                js = slice(h * P, (h + 1) * P)
+                turned = keep.tile([P, PACK, P], F32, name=f"turned{h}")
+                nc.scalar.copy(turned[:], sums_t[h][:])
+                back = psum.tile([P, PACK, P], F32, name=f"back{h}", tag=f"sum{h}")
+                for t in range(PACK):
+                    nc.tensor.transpose(back[:, t, :], turned[:, t, :], ident[:])
+                nc.scalar.copy(y[:, :, js], back[:])
+            nc.sync.dma_start(y_rows[:, :, j0 : j0 + w], y[:])
+            nc.scalar.copy(y_bf[:], y[:].rearrange("p t j -> p j t"))
+            return y_bf
+
         def pool_up(u):
             seg, c = units[u]
             j0, w, mode = seg
             last = c == PICKS - 1
-            closing = PICKS - 1 if mode == "tensor" else PICKS - 2
             prod = keep.tile([P, w // P, PACK, P], F32, name=f"prod{u}")
-            if last:
-                y = keep.tile([P, PACK, w], F32, name=f"y{j0}")
+            if last and mode != "tensor":
                 y_bf = keep.tile([P, w, PACK], BF16, name=f"y_bf{j0}", align_bytes=64)
             for h, acc in enumerate(banks[u]):
                 js = slice(h * P, (h + 1) * P)
-                tile_j = j0 // P + h
                 nc.vector.tensor_tensor(prod[:, h, :, :], acc[:], iw_sb[u][:, :, js], MULT)
-                if c <= closing:
+                if mode == "tensor":
                     for t in range(PACK):
                         nc.tensor.matmul(
-                            sums_t[tile_j][:, t, :], prod[:, h, t, :], ident[:], is_transpose=True,
-                            start=False, stop=(c == closing and t == PACK - 1),
+                            sums_t[h][:, t, :], prod[:, h, t, :], ident[:], is_transpose=True,
+                            start=False, stop=(last and t == PACK - 1),
                         )
-                if c == closing:
-                    turned = keep.tile([P, PACK, P], F32, name=f"turned{tile_j}")
-                    nc.scalar.copy(turned[:], sums_t[tile_j][:])
-                    back = psum.tile([P, PACK, P], F32, name=f"back{tile_j}", tag=f"sum{tile_j}")
-                    prods[tile_j] = back
-                    for t in range(PACK):
-                        nc.tensor.transpose(back[:, t, :], turned[:, t, :], ident[:])
-                if last:
-                    if mode == "tensor":
-                        nc.scalar.copy(y[:, :, js], prods[tile_j][:])
-                    else:
-                        nc.vector.tensor_tensor(y[:, :, js], prods[tile_j][:], prod[:, h, :, :], ADD)
-                        nc.sync.dma_start(y_rows[:, :, j0 + h * P : j0 + (h + 1) * P], y[:, :, js])
-                    copy = nc.vector.tensor_copy if tile_j == J // P - 1 else nc.scalar.copy
-                    copy(y_bf[:, js, :], y[:, :, js].rearrange("p t j -> p j t"))
+            if mode == "tensor":
+                return
+            total = keep.tile([P, w // P, PACK, P], F32, name=f"total{u}")
+            if c == 0:
+                for t in range(PACK):
+                    nc.scalar.activation(total[:, :, t, :], prod[:, :, t, :], IDENTITY, bias=bias[:, t : t + 1])
+            else:
+                for h in range(w // P):
+                    js = slice(h * P, (h + 1) * P)
+                    nc.vector.tensor_tensor(total[:, h, :, :], prods[u - 1][:, h, :, :], prod[:, h, :, :], ADD)
+                    if last:
+                        nc.sync.dma_start(y_rows[:, :, j0 + h * P : j0 + (h + 1) * P], total[:, h, :, :])
+                        copy = nc.scalar.copy if h < w // P - 1 else nc.vector.tensor_copy
+                        copy(y_bf[:, js, :], total[:, h, :, :].rearrange("p t j -> p j t"))
+            prods[u] = total
             if last:
-                if mode == "tensor":
-                    nc.sync.dma_start(y_rows[:, :, j0 : j0 + w], y[:])
                 hand_out(seg, y_bf)
 
-        for step in range(len(units) + 2):
+        for step in range(len(units) + 3):
             if step < len(units):
                 pick(step)
             if 1 <= step <= len(units):
+                quantise(step - 1)
+            if step >= 3:
+                pool_up(step - 3)
+            if 1 <= step <= len(units):
                 project(step - 1)
-            if step >= 2:
-                pool_up(step - 2)
+            if step == 6:
+                first_bf = turn_back(SEGMENTS[0])
+            if step == 7:
+                hand_out(SEGMENTS[0], first_bf)
 
         for q in range(4):
             queue = nc.sync if q % 2 == 0 else nc.scalar

from contextlib import ExitStack

import concourse.mybir as mybir
from concourse.masks import make_identity

FLOPS = 1610612736

F32 = mybir.dt.float32
BF16 = mybir.dt.bfloat16
I32 = mybir.dt.int32
U32 = mybir.dt.uint32
U16 = mybir.dt.uint16
U8 = mybir.dt.uint8
FP8X4 = mybir.dt.float8_e4m3fn_x4
FP4X4 = mybir.dt.float4_e2m1fn_x4
MULT = mybir.AluOpType.mult
ADD = mybir.AluOpType.add
IDENTITY = mybir.ActivationFunctionType.Identity

P = 128
PACK = 4
N = 512
T = 2048
J = 512
PICKS = 3
LIST_ROWS = 16
BANK = 512

SEGMENTS = ((0, 256, "tensor"), (256, 256, "vector"))
AHEAD = 3


def tile_list_dl_soft_biasP_kernel(
    tc, xT, wgt, w4_words, w4_scales, wd, iw0, iw1, iw2, b, offs, out_0, out_1, out_2
):
    nc = tc.nc
    iw = (iw0, iw1, iw2)
    units = [(seg, c) for seg in SEGMENTS for c in range(PICKS)]

    with ExitStack() as ctx:
        keep = ctx.enter_context(tc.tile_pool(name="keep", bufs=1))
        psum = ctx.enter_context(tc.psum_pool(name="psum", bufs=1))

        offsets = keep.tile([P, PICKS * J // LIST_ROWS], U16, name="offsets")
        nc.sync.dma_start(offsets[:], offs)
        s4_raw = keep.tile([P, N], U8, name="s4_raw")
        nc.vector.memset(s4_raw[:].bitcast(I32), 0)
        wgt_pieces = wgt.rearrange("(g q) (r m) -> g q r m", q=LIST_ROWS, m=P)[:, 0, :, :]
        wgt_rows = [keep.tile([P, P], F32, name=f"wgt_rows{k}") for k in range(2)]
        nc.vector.memset(wgt_rows[0][64:128, :], 0.0)
        nc.vector.memset(wgt_rows[1][32:64, :], 0.0)
        nc.vector.memset(wgt_rows[1][64:128, :], 0.0)
        nc.sync.dma_start(wgt_rows[0][0:64, :], wgt_pieces[:, 0:8, :])

        w4_raw = keep.tile([P, 2 * N], U8, name="w4_raw")
        nc.sync.dma_start(w4_raw[:].bitcast(I32), w4_words[0].bitcast(I32))

        x_planes = xT.rearrange("(p i) t -> p i t", i=PACK)
        wgt_sb = [keep.tile([P, J], F32, name=f"wgt{c}") for c in range(PICKS)]
        plane = [keep.tile([P, T], F32, name=f"plane{i}") for i in range(PACK)]
        wd_raw = keep.tile([P, PACK, N], F32, name="wd_raw")
        bias = keep.tile([P, PACK], F32, name="bias")
        nc.sync.dma_start(plane[0][:], x_planes[:, 0, :])
        nc.sync.dma_start(wgt_rows[1][0:32, :], wgt_pieces[:, 8:12, :])
        nc.sync.dma_start(bias[:], b.rearrange("(p t) -> p t", t=PACK))
        nc.sync.dma_start(plane[1][:], x_planes[:, 1, :])
        for q in range(4):
            nc.sync.dma_start(s4_raw[32 * q : 32 * q + 4, :].bitcast(I32), w4_scales[0, 4 * q : 4 * q + 4, :].bitcast(I32))
        nc.sync.dma_start(wd_raw[:], wd.rearrange("(p i) n -> p i n", i=PACK))
        nc.sync.dma_start(plane[2][:], x_planes[:, 2, :])
        nc.sync.dma_start(plane[3][:], x_planes[:, 3, :])
        iw_sb = []
        for u, ((j0, w, mode), c) in enumerate(units):
            t_iw = keep.tile([P, PACK, w], F32, name=f"iw{u}", tag=f"iw_slot{u}", align_bytes=64)
            nc.sync.dma_start(t_iw[:], iw[c].rearrange("(p t) j -> p t j", t=PACK)[:, :, j0 : j0 + w])
            iw_sb.append(t_iw)

        ident = keep.tile([P, P], F32, name="ident")
        make_identity(nc, ident[:])
        warm = keep.tile([P, 1], F32, name="warm")
        nc.scalar.copy(warm[:], ident[:, 0:1])

        for c in range(PICKS):
            if c % 2 == 0:
                by_place = psum.tile([P, P], F32, name=f"by_place{c}", tag="sum0")
                nc.tensor.transpose(by_place[:], wgt_rows[c // 2][:], ident[:])
                runs = 8 if c == 0 else 4
                pieces = by_place[:, 0 : 8 * runs].rearrange("m (g r) -> m r g", r=runs)
            spread = keep.tile([P, PACK, 8, LIST_ROWS], F32, name=f"spread{c}")
            nc.scalar.copy(spread[:], pieces[:, PACK * (c % 2) : PACK * (c % 2 + 1), :].unsqueeze(3).to_broadcast([P, PACK, 8, LIST_ROWS]))
            turned_back = psum.tile([P, PACK, P], F32, name=f"wgt_ps{c}", tag="sum1")
            for r in range(PACK):
                nc.tensor.transpose(turned_back[:, r, :], spread[:, r, :, :].rearrange("m g q -> m (g q)"), ident[:])
            nc.scalar.copy(wgt_sb[c][:], turned_back[:].rearrange("p r m -> p (r m)"))
        sums_t = []
        for h in range(2):
            sum_t = psum.tile([P, PACK, P], F32, name=f"sum_t{h}", tag=f"sum{h}")
            sums_t.append(sum_t)
            for t in range(PACK):
                nc.tensor.matmul(
                    sum_t[:, t, :], bias[:, t : t + 1].to_broadcast([P, P]), ident[:], is_transpose=True,
                    start=(t == 0), stop=False,
                )

        w4_codes = keep.tile([P, 2 * N], U8, name="w4_codes", align_bytes=64)
        nc.vector.tensor_copy(
            w4_codes[:].rearrange("p (t m e) -> p t m e", t=PACK, e=2),
            w4_raw[:].rearrange("p (m t e) -> p t m e", t=PACK, e=2),
        )

        def gather(dst, i, c, j0, w):
            first = (c * J + j0) // LIST_ROWS
            picks = offsets[:, first : first + w // LIST_ROWS]
            nc.vector.tensor_tensor(dst, plane[i][:].indirect(picks), wgt_sb[c][:, j0 : j0 + w], MULT)

        low = [keep.tile([P, 2, J], F32, name=f"low{c}") for c in range(PICKS)]
        for i in range(2):
            for c in range(PICKS):
                gather(low[c][:, i, :], i, c, 0, J)

        wd_bf = keep.tile([P, PACK, P, PACK], BF16, name="wd_bf", align_bytes=64)
        nc.scalar.copy(
            wd_bf[:].rearrange("p t m i -> p m t i"),
            wd_raw[:].rearrange("p i (m t) -> p m t i", t=PACK),
        )
        wd_codes = keep.tile([P, N], U32, name="wd_codes", align_bytes=64)
        wd_plane = keep.tile([P, N], U8, name="wd_plane", align_bytes=64)
        nc.vector.quantize_mx(wd_codes[:].bitcast(FP8X4), wd_plane[:], wd_bf[:].rearrange("p t m i -> p (t m i)"))

        w4_plane = keep.tile([P, N], U8, name="w4_plane", tag="wd_bf", align_bytes=64)
        nc.vector.tensor_copy(
            w4_plane[:].rearrange("p (t m) -> p t m", t=PACK),
            s4_raw[:].rearrange("p (m t) -> p t m", t=PACK),
        )
        xg_bf = {}

        y_plane = keep.tile([P, J], U8, name="y_plane", align_bytes=64)
        y_rows = out_0.rearrange("(p t) j -> p t j", t=PACK)
        y_words = out_1[0].rearrange("p j i -> p (j i)").bitcast(I32)
        banks = {}
        quantised = {}
        prods = {}

        def pick(u):
            (j0, w, mode), c = units[u]
            xg_bf[u] = keep.tile([P, w, PACK], BF16, name=f"xg_bf{u}", tag=("slot0", "slot1", "slot2", "first1", "first0", "slot2")[u], align_bytes=64)
            nc.scalar.copy(xg_bf[u][:, :, 0:2], low[c][:, :, j0 : j0 + w].rearrange("p i j -> p j i"))
            tag = ("first0", "first1", "first0", "slot1", "iw_slot0", "iw_slot1")[u]
            high = keep.tile([P, 2, w], F32, name=f"high{u}", tag=tag, align_bytes=64)
            for i in range(2):
                gather(high[:, i, :], 2 + i, c, j0, w)
            nc.scalar.copy(xg_bf[u][:, :, 2:4], high[:].rearrange("p i j -> p j i"))

        def quantise(u):
            (j0, w, mode), c = units[u]
            codes = keep.tile([P, w], U32, name=f"xg_codes{u}", align_bytes=64)
            scales = keep.tile([P, w], U8, name=f"xg_plane{u}", align_bytes=64)
            nc.vector.quantize_mx(codes[:].bitcast(FP8X4), scales[:], xg_bf[u][:].rearrange("p j i -> p (j i)"))
            quantised[u] = (codes, scales)

        def project(u):
            (j0, w, mode), c = units[u]
            codes, scales = quantised[u]
            banks[u] = []
            for h in range(w // P):
                acc = psum.tile([P, PACK, P], F32, name=f"acc{u}_{h}", tag="acc", bufs=6)
                banks[u].append(acc)
                js = slice(h * P, (h + 1) * P)
                for t in range(PACK):
                    cols = slice(t * P, (t + 1) * P)
                    nc.tensor.matmul_mx(
                        acc[:, t, :], wd_codes[:, cols].bitcast(FP8X4), wd_plane[:, cols],
                        codes[:, js].bitcast(FP8X4), scales[:, js], start=True, stop=False,
                    )
                    nc.tensor.matmul_mx(
                        acc[:, t, :], w4_codes[:, 2 * t * P : 2 * (t + 1) * P].bitcast(FP4X4), w4_plane[:, cols],
                        codes[:, js].bitcast(FP8X4), scales[:, js], start=False, stop=True,
                    )

        def hand_out(seg, y_bf):
            j0, w, mode = seg
            y_codes = keep.tile([P, w], U32, name=f"y_codes{j0}", align_bytes=64)
            piece = w if mode == "tensor" else P
            for first in range(0, w, piece):
                js = slice(first, first + piece)
                nc.vector.quantize_mx(
                    y_codes[:, js].bitcast(FP8X4), y_plane[:, j0 + first : j0 + first + piece],
                    y_bf[:, js, :].rearrange("p j t -> p (j t)"),
                )
            nc.sync.dma_start(y_words[:, j0 : j0 + w], y_codes[:].bitcast(I32))

        def turn_back(seg):
            j0, w, mode = seg
            y = keep.tile([P, PACK, w], F32, name=f"y{j0}")
            y_bf = keep.tile([P, w, PACK], BF16, name=f"y_bf{j0}", align_bytes=64)
            for h in range(w // P):
                js = slice(h * P, (h + 1) * P)
                turned = keep.tile([P, PACK, P], F32, name=f"turned{h}")
                nc.scalar.copy(turned[:], sums_t[h][:])
                back = psum.tile([P, PACK, P], F32, name=f"back{h}", tag=f"sum{h}")
                for t in range(PACK):
                    nc.tensor.transpose(back[:, t, :], turned[:, t, :], ident[:])
                nc.scalar.copy(y[:, :, js], back[:])
            nc.sync.dma_start(y_rows[:, :, j0 : j0 + w], y[:])
            nc.scalar.copy(y_bf[:], y[:].rearrange("p t j -> p j t"))
            return y_bf

        def pool_up(u):
            seg, c = units[u]
            j0, w, mode = seg
            last = c == PICKS - 1
            prod = keep.tile([P, w // P, PACK, P], F32, name=f"prod{u}")
            if last and mode != "tensor":
                y_bf = keep.tile([P, w, PACK], BF16, name=f"y_bf{j0}", align_bytes=64)
            for h, acc in enumerate(banks[u]):
                js = slice(h * P, (h + 1) * P)
                nc.vector.tensor_tensor(prod[:, h, :, :], acc[:], iw_sb[u][:, :, js], MULT)
                if mode == "tensor":
                    for t in range(PACK):
                        nc.tensor.matmul(
                            sums_t[h][:, t, :], prod[:, h, t, :], ident[:], is_transpose=True,
                            start=False, stop=(last and t == PACK - 1),
                        )
            if mode == "tensor":
                return
            total = keep.tile([P, w // P, PACK, P], F32, name=f"total{u}")
            if c == 0:
                for t in range(PACK):
                    nc.scalar.activation(total[:, :, t, :], prod[:, :, t, :], IDENTITY, bias=bias[:, t : t + 1])
            else:
                for h in range(w // P):
                    js = slice(h * P, (h + 1) * P)
                    nc.vector.tensor_tensor(total[:, h, :, :], prods[u - 1][:, h, :, :], prod[:, h, :, :], ADD)
                    if last:
                        nc.sync.dma_start(y_rows[:, :, j0 + h * P : j0 + (h + 1) * P], total[:, h, :, :])
                        copy = nc.scalar.copy if h < w // P - 1 else nc.vector.tensor_copy
                        copy(y_bf[:, js, :], total[:, h, :, :].rearrange("p t j -> p j t"))
            prods[u] = total
            if last:
                hand_out(seg, y_bf)

        for step in range(len(units) + 3):
            if step < len(units):
                pick(step)
            if 1 <= step <= len(units):
                quantise(step - 1)
            if step >= 3:
                pool_up(step - 3)
            if 1 <= step <= len(units):
                project(step - 1)
            if step == 6:
                first_bf = turn_back(SEGMENTS[0])
            if step == 7:
                hand_out(SEGMENTS[0], first_bf)

        for q in range(4):
            queue = nc.sync if q % 2 == 0 else nc.scalar
            queue.dma_start(out_2[0, 4 * q : 4 * q + 4, :].bitcast(I32), y_plane[32 * q : 32 * q + 4, :].bitcast(I32))
